import numpy as np
import ml_dtypes


def mxq(x, axis, fmt="e4m3"):
    dtype, down = {"e4m3": (ml_dtypes.float8_e4m3fn, 7), "e5m2": (ml_dtypes.float8_e5m2, 14)}[fmt]
    v = np.moveaxis(np.asarray(x, np.float32).astype(ml_dtypes.bfloat16).astype(np.float64), axis, -1)
    blocks = v.reshape(v.shape[:-1] + (-1, 32))
    amax = np.abs(blocks).max(-1, keepdims=True)
    byte = np.maximum(np.where(amax > 0, np.frexp(amax)[1] - 1 + 127, 0) - down, 1)
    scale = np.exp2(byte - 127.0)
    codes = (blocks / scale).astype(np.float32).astype(dtype).astype(np.float64)
    return np.moveaxis((codes * scale).reshape(v.shape), -1, axis)


WIDE = False


def mx_kscale(k):
    if not WIDE:
        return np.ones(k)
    levels = np.array([30, -30])
    if k % 512:
        return np.exp2(np.random.permutation(np.resize(levels, k // 32))).repeat(32)
    a = np.empty((k // 512, 16))
    for p in range(k // 512):
        a[p, :8] = np.random.permutation(np.resize(levels, 8))
        for g in range(8):
            far = levels[np.abs(levels - a[p, g]) >= 10]
            a[p, g + 8] = far[np.random.randint(len(far))]
    return np.exp2(a.ravel()).repeat(32)


def f64(x):
    return np.asarray(x).astype(np.float64)


def striped(idx):
    return np.tile(np.asarray(idx).reshape(-1, 16).T, (8, 1)).astype(np.uint16)


def unstriped(offs):
    return offs[:16].T.reshape(-1).astype(np.int64)


E2M1 = np.array([0.0, 0.5, 1.0, 1.5, 2.0, 3.0, 4.0, 6.0, -0.0, -0.5, -1.0, -1.5, -2.0, -3.0, -4.0, -6.0])


def pack_weight(w, fmt):
    k, n = w.shape
    w = f64(np.asarray(w, np.float32).astype(ml_dtypes.bfloat16)).reshape(k // 32, 32, n)
    amax = np.abs(w).max(1)
    if fmt in ("e4m3", "e5m2"):
        byte = np.frexp(amax)[1] - 1 + 127 - (7 if fmt == "e4m3" else 14)
    else:
        mant, ex = np.frexp(amax / 6.0)
        byte = np.where(mant > 0.5, ex, ex - 1) + 127
    byte = np.clip(np.where(amax > 0, byte, 1), 1, 254)
    scaled = (w * np.exp2(127.0 - byte)[:, None, :]).reshape(k, n).astype(np.float32)
    by_word = np.ascontiguousarray(scaled.reshape(k // 512, 128, 4, n).transpose(0, 1, 3, 2))
    if fmt in ("e4m3", "e5m2"):
        words = by_word.astype(ml_dtypes.float8_e4m3fn if fmt == "e4m3" else ml_dtypes.float8_e5m2).view(np.uint8)
    else:
        c = by_word.astype(ml_dtypes.float4_e2m1fn).view(np.uint8) & 0xF
        words = (c[..., 0::2] | (c[..., 1::2] << 4)).reshape(k // 512, 128, 2 * n)
    return np.ascontiguousarray(words), np.ascontiguousarray(byte.astype(np.uint8).reshape(k // 512, 16, n))


def unpack_weight(words, scales, fmt):
    g, _, n = scales.shape
    words = np.ascontiguousarray(words).reshape(g, 128, n, -1)
    if fmt in ("e4m3", "e5m2"):
        vals = words.view(ml_dtypes.float8_e4m3fn if fmt == "e4m3" else ml_dtypes.float8_e5m2).astype(np.float64)
    else:
        nib = np.empty((g, 128, n, 4), np.uint8)
        nib[..., 0::2] = words & 0xF
        nib[..., 1::2] = words >> 4
        vals = E2M1[nib]
    vals = vals * np.repeat(np.exp2(scales.astype(np.float64) - 127.0), 8, axis=1)[..., None]
    return vals.transpose(0, 1, 3, 2).reshape(g * 512, n)


K, T, Z, J, R, C, O, N = 512, 1024, 1024, 256, 512, 512, 256, 256


def setup_inputs():
    n = np.random.standard_normal
    idx = np.random.permutation(T)[:J]
    idx2 = np.random.permutation(Z)[:J]
    idx3 = np.random.permutation(C)[:J]
    idx4 = np.random.permutation(C)[:J]
    idx5 = np.random.permutation(C)[:O]
    fk = mx_kscale(K)
    fr = mx_kscale(R)
    xtp = pack_weight(n((K, T)) / fk[:, None], "e4m3")
    xop = pack_weight(n((K, Z)) / fk[:, None], "e2m1")
    wp = pack_weight(n((K, R)) * 1 / np.sqrt(K) * fk[:, None] * fr, "e5m2")
    wbp = pack_weight(n((R, N)) * 1 / np.sqrt(R) / fr[:, None], "e5m2")
    return {
        "xt_words": xtp[0],
        "xt_scales": xtp[1],
        "xo_words": xop[0],
        "xo_scales": xop[1],
        "w_words": wp[0],
        "w_scales": wp[1],
        "wb_words": wbp[0],
        "wb_scales": wbp[1],
        "offs": striped(idx),
        "offs2": striped(idx2),
        "offs3": striped(idx3),
        "offs4": striped(idx4),
        "offs5": striped(idx5),
    }


def reference(xt_words, xt_scales, xo_words, xo_scales, w_words, w_scales, wb_words, wb_scales, offs, offs2, offs3, offs4, offs5):
    idx = unstriped(offs)
    idx2 = unstriped(offs2)
    idx3 = unstriped(offs3)
    idx4 = unstriped(offs4)
    idx5 = unstriped(offs5)
    xtu = unpack_weight(xt_words, xt_scales, "e4m3")
    xou = unpack_weight(xo_words, xo_scales, "e2m1")
    wu = unpack_weight(w_words, w_scales, "e5m2")
    wbu = unpack_weight(wb_words, wb_scales, "e5m2")
    xtidxg = xtu[:, idx]
    a = wu.T @ xtidxg
    xoidx2g = xou[:, idx2]
    b = wu.T @ xoidx2g
    pw = np.zeros((R, C))
    pw[:, idx3] = a
    pv = np.zeros((R, C))
    pv[:, idx4] = b
    pg = pw + pv
    hid = pg[:, idx5]
    hidq = mxq(hid, 0, "e4m3")
    y = wbu.T @ hidq
    return y

@@ -1,0 +1,172 @@
+from contextlib import ExitStack
+
+import concourse.mybir as mybir
+
+K, T, Z, J, R, C, O, N = 512, 1024, 1024, 256, 512, 512, 256, 256
+FLOPS = 2 * (2 * K * R * J + R * N * O)
+
+F32 = mybir.dt.float32
+BF16 = mybir.dt.bfloat16
+I32 = mybir.dt.int32
+U32 = mybir.dt.uint32
+U16 = mybir.dt.uint16
+U8 = mybir.dt.uint8
+E4M3 = mybir.dt.float8_e4m3fn_x4
+E5M2 = mybir.dt.float8_e5m2_x4
+E2M1 = mybir.dt.float4_e2m1fn_x4
+COPY = mybir.ActivationFunctionType.Copy
+ADD = mybir.AluOpType.add
+
+P = 128
+PACK = 4
+
+
+def tile_list_oneforboth_shared_one_plain_kernel(
+    tc, xt_words, xt_scales, xo_words, xo_scales, w_words, w_scales, wb_words, wb_scales,
+    offs, offs2, offs3, offs4, offs5, out,
+):
+    nc = tc.nc
+    with ExitStack() as ctx:
+        sb = ctx.enter_context(tc.tile_pool(name="sb", bufs=1))
+        ps = ctx.enter_context(tc.psum_pool(name="ps", bufs=1))
+
+        def tile(name, cols, dtype):
+            return sb.tile([P, cols], dtype, name=name, align_bytes=64)
+
+        l_xt = tile("l_xt", J // 16, U16)
+        l_xo = tile("l_xo", J // 16, U16)
+        l_a = tile("l_a", J // 16, U16)
+        l_b = tile("l_b", J // 16, U16)
+        l_hid = tile("l_hid", O // 16, U16)
+
+        xt_w, xt_s = tile("xt_w", T, U32), tile("xt_s", T, U8)
+        xo_w, xo_s = tile("xo_w", Z, U16), tile("xo_s", Z, U8)
+        w_w, w_s = tile("w_w", R, U32), tile("w_s", R, U8)
+        wb_w, wb_s = tile("wb_w", N, U32), tile("wb_s", N, U8)
+        xtg_w, xtg_s = tile("xtg_w", J, U32), tile("xtg_s", J, U8)
+        xog_w, xog_s = tile("xog_w", J, U16), tile("xog_s", J, U8)
+        wp_w, wp_s = tile("wp_w", R, U32), tile("wp_s", R, U8)
+        pw = [tile("pw%d" % t, C, F32) for t in range(PACK)]
+        pv = [tile("pv%d" % t, C, F32) for t in range(PACK)]
+        pg = [tile("pg%d" % t, C, F32) for t in range(PACK)]
+        a_sb = [tile("a%d" % t, J, F32) for t in range(PACK)]
+        b_sb = [tile("b%d" % t, J, F32) for t in range(PACK)]
+        hid = tile("hid", O * PACK, BF16)
+        hq_w, hq_s = tile("hq_w", O, U32), tile("hq_s", O, U8)
+
+        def load_words(queue, dst, src):
+            queue.dma_start(out=dst[:].bitcast(I32), in_=src.bitcast(I32))
+
+        def load_scale_rows(queue, dst, src, q):
+            rows = src[0, 4 * q : 4 * q + 4, :].bitcast(I32)
+            queue.dma_start(
+                out=dst[32 * q : 32 * (q + 1), :].bitcast(I32),
+                in_=rows.unsqueeze(0).broadcast_to([8, 4, rows.shape[1]]),
+            )
+
+        nc.sync.dma_start(out=l_xo[:], in_=offs2)
+        for q in range(2):
+            load_scale_rows(nc.scalar, w_s, w_scales, q)
+        load_words(nc.scalar, w_w, w_words[0].rearrange("p n t -> p (n t)"))
+        load_words(nc.scalar, xo_w, xo_words[0])
+        load_words(nc.scalar, xt_w, xt_words[0].rearrange("p n t -> p (n t)"))
+        for q in range(4):
+            load_scale_rows(nc.sync, xo_s, xo_scales, q)
+        for q in range(2, 4):
+            load_scale_rows(nc.sync, w_s, w_scales, q)
+        nc.sync.dma_start(out=l_b[:], in_=offs4)
+        nc.sync.dma_start(out=l_xt[:], in_=offs)
+        for q in range(4):
+            load_scale_rows(nc.sync, xt_s, xt_scales, q)
+        nc.sync.dma_start(out=l_a[:], in_=offs3)
+        nc.sync.dma_start(out=l_hid[:], in_=offs5)
+        load_words(nc.sync, wb_w, wb_words[0].rearrange("p n t -> p (n t)"))
+        for q in range(4):
+            load_scale_rows(nc.sync, wb_s, wb_scales, q)
+
+        for t in range(PACK):
+            nc.vector.memset(pv[t][:], 0.0)
+        for t in range(PACK):
+            nc.gpsimd.memset(pw[t][:], 0.0)
+
+        nc.vector.tensor_copy(
+            out=wp_w[:].rearrange("p (t g i) -> p g t i", t=PACK, i=4),
+            in_=w_w[:].rearrange("p (g i t) -> p g t i", t=PACK, i=4),
+        )
+        nc.vector.tensor_copy(out=xog_w[:], in_=xo_w[:].indirect(l_xo[:]))
+        nc.vector.tensor_copy(out=xog_s[:], in_=xo_s[:].indirect(l_xo[:]))
+        nc.vector.tensor_copy(
+            out=wp_s[:].rearrange("p (t m) -> p t m", t=PACK),
+            in_=w_s[:].rearrange("p (m t) -> p t m", t=PACK),
+        )
+
+        def first_product(name, t, words, scales):
+            acc = ps.tile([P, J], F32, name=name, tag=name)
+            cols = slice(P * t, P * (t + 1))
+            nc.tensor.matmul_mx(
+                out=acc[:], lhsT=wp_w[:, cols].bitcast(E5M2), lhsT_scale=wp_s[:, cols],
+                rhs=words, rhs_scale=scales, start=True, stop=True,
+            )
+            return acc
+
+        b_ps = [first_product("b_ps%d" % t, t, xog_w[:].bitcast(E2M1), xog_s[:]) for t in range(PACK)]
+
+        nc.vector.tensor_copy(out=xtg_w[:], in_=xt_w[:].indirect(l_xt[:]))
+
+        def drain_s(dst, src):
+            nc.scalar.activation(out=dst[:], in_=src[:], func=COPY)
+
+        def put_s(page, lst, src):
+            nc.scalar.activation(out=page[:].indirect(lst[:]), in_=src[:], func=COPY)
+
+        def put_v(page, lst, src):
+            nc.vector.tensor_copy(out=page[:].indirect(lst[:]), in_=src[:])
+
+        hid_t = hid[:].rearrange("p (o t) -> p t o", t=PACK)
+
+        def read_board(t):
+            nc.vector.tensor_tensor(out=pg[t][:], in0=pw[t][:], in1=pv[t][:], op=ADD)
+            nc.vector.tensor_copy(out=hid_t[:, t, :], in_=pg[t][:].indirect(l_hid[:]))
+
+        def drain_v(dst, src):
+            nc.vector.tensor_copy(out=dst[:], in_=src[:])
+
+        drain_s(b_sb[0], b_ps[0])
+        drain_v(b_sb[1], b_ps[1])
+        put_s(pv[0], l_b, b_sb[0])
+        put_v(pv[1], l_b, b_sb[1])
+        drain_s(b_sb[2], b_ps[2])
+        put_s(pv[2], l_b, b_sb[2])
+        nc.vector.tensor_copy(out=xtg_s[:], in_=xt_s[:].indirect(l_xt[:]))
+        a_ps = [first_product("a_ps%d" % t, t, xtg_w[:].bitcast(E4M3), xtg_s[:]) for t in range(PACK)]
+        drain_v(b_sb[3], b_ps[3])
+        drain_v(a_sb[0], a_ps[0])
+        put_v(pw[0], l_a, a_sb[0])
+        put_s(pv[3], l_b, b_sb[3])
+        read_board(0)
+        drain_s(a_sb[1], a_ps[1])
+        drain_s(a_sb[2], a_ps[2])
+        put_s(pw[2], l_a, a_sb[2])
+        put_v(pw[1], l_a, a_sb[1])
+        read_board(1)
+        drain_s(a_sb[3], a_ps[3])
+        put_s(pw[3], l_a, a_sb[3])
+        read_board(2)
+        read_board(3)
+
+        nc.vector.quantize_mx(out=hq_w[:].bitcast(E4M3), scales=hq_s[:], in_=hid[:])
+
+        for h in range(N // P):
+            cols = slice(P * h, P * (h + 1))
+            y_ps = ps.tile([P, O], F32, name="y_ps%d" % h, tag="b_ps%d" % h)
+            nc.tensor.matmul_mx(
+                out=y_ps[:], lhsT=wb_w[:, cols].bitcast(E5M2), lhsT_scale=wb_s[:, cols],
+                rhs=hq_w[:].bitcast(E4M3), rhs_scale=hq_s[:], start=True, stop=True,
+            )
+            y_sb = tile("y%d" % h, O, F32)
+            if h == 0:
+                nc.vector.tensor_copy(out=y_sb[:], in_=y_ps[:])
+                nc.sync.dma_start(out=out[cols, :], in_=y_sb[:])
+            else:
+                drain_s(y_sb, y_ps)
+                nc.scalar.dma_start(out=out[cols, :], in_=y_sb[:])

@@ -30,8 +30,8 @@ def tile_list_oneforboth_shared_one_plain_kernel(
         sb = ctx.enter_context(tc.tile_pool(name="sb", bufs=1))
         ps = ctx.enter_context(tc.psum_pool(name="ps", bufs=1))
 
-        def tile(name, cols, dtype):
-            return sb.tile([P, cols], dtype, name=name, align_bytes=64)
+        def tile(name, cols, dtype, tag=None):
+            return sb.tile([P, cols], dtype, name=name, tag=tag or name, align_bytes=64)
 
         l_xt = tile("l_xt", J // 16, U16)
         l_xo = tile("l_xo", J // 16, U16)
@@ -50,7 +50,7 @@ def tile_list_oneforboth_shared_one_plain_kernel(
         pv = [tile("pv%d" % t, C, F32) for t in range(PACK)]
         pg = [tile("pg%d" % t, C, F32) for t in range(PACK)]
         a_sb = [tile("a%d" % t, J, F32) for t in range(PACK)]
-        b_sb = [tile("b%d" % t, J, F32) for t in range(PACK)]
+        b_sb = {t: tile("b%d" % t, J, F32) for t in (0, 2, 3)}
         hid = tile("hid", O * PACK, BF16)
         hq_w, hq_s = tile("hq_w", O, U32), tile("hq_s", O, U8)
 
@@ -65,17 +65,16 @@ def tile_list_oneforboth_shared_one_plain_kernel(
             )
 
         nc.sync.dma_start(out=l_xo[:], in_=offs2)
-        for q in range(2):
-            load_scale_rows(nc.scalar, w_s, w_scales, q)
-        load_words(nc.scalar, w_w, w_words[0].rearrange("p n t -> p (n t)"))
-        load_words(nc.scalar, xo_w, xo_words[0])
-        load_words(nc.scalar, xt_w, xt_words[0].rearrange("p n t -> p (n t)"))
         for q in range(4):
+            load_scale_rows(nc.scalar, w_s, w_scales, q)
+        load_scale_rows(nc.sync, xo_s, xo_scales, 0)
+        load_words(nc.sync, w_w, w_words[0].rearrange("p n t -> p (n t)"))
+        load_words(nc.sync, xo_w, xo_words[0])
+        for q in range(1, 4):
             load_scale_rows(nc.sync, xo_s, xo_scales, q)
-        for q in range(2, 4):
-            load_scale_rows(nc.sync, w_s, w_scales, q)
-        nc.sync.dma_start(out=l_b[:], in_=offs4)
+        load_words(nc.sync, xt_w, xt_words[0].rearrange("p n t -> p (n t)"))
         nc.sync.dma_start(out=l_xt[:], in_=offs)
+        nc.sync.dma_start(out=l_b[:], in_=offs4)
         for q in range(4):
             load_scale_rows(nc.sync, xt_s, xt_scales, q)
         nc.sync.dma_start(out=l_a[:], in_=offs3)
@@ -90,18 +89,18 @@ def tile_list_oneforboth_shared_one_plain_kernel(
             nc.gpsimd.memset(pw[t][:], 0.0)
 
         nc.vector.tensor_copy(
+            out=wp_s[:].rearrange("p (t m) -> p t m", t=PACK),
+            in_=w_s[:].rearrange("p (m t) -> p t m", t=PACK),
+        )
+        nc.vector.tensor_copy(
             out=wp_w[:].rearrange("p (t g i) -> p g t i", t=PACK, i=4),
             in_=w_w[:].rearrange("p (g i t) -> p g t i", t=PACK, i=4),
         )
         nc.vector.tensor_copy(out=xog_w[:], in_=xo_w[:].indirect(l_xo[:]))
         nc.vector.tensor_copy(out=xog_s[:], in_=xo_s[:].indirect(l_xo[:]))
-        nc.vector.tensor_copy(
-            out=wp_s[:].rearrange("p (t m) -> p t m", t=PACK),
-            in_=w_s[:].rearrange("p (m t) -> p t m", t=PACK),
-        )
 
-        def first_product(name, t, words, scales):
-            acc = ps.tile([P, J], F32, name=name, tag=name)
+        def first_product(name, bank, t, words, scales):
+            acc = ps.tile([P, J], F32, name=name, tag=bank)
             cols = slice(P * t, P * (t + 1))
             nc.tensor.matmul_mx(
                 out=acc[:], lhsT=wp_w[:, cols].bitcast(E5M2), lhsT_scale=wp_s[:, cols],
@@ -109,64 +108,76 @@ def tile_list_oneforboth_shared_one_plain_kernel(
             )
             return acc
 
-        b_ps = [first_product("b_ps%d" % t, t, xog_w[:].bitcast(E2M1), xog_s[:]) for t in range(PACK)]
+        b_ps = [first_product("b_ps%d" % t, "b_ps%d" % t, t, xog_w[:].bitcast(E2M1), xog_s[:]) for t in range(PACK - 1)]
 
         nc.vector.tensor_copy(out=xtg_w[:], in_=xt_w[:].indirect(l_xt[:]))
 
         def drain_s(dst, src):
-            nc.scalar.activation(out=dst[:], in_=src[:], func=COPY)
+            nc.scalar.activation(out=dst, in_=src, func=COPY)
+
+        def drain_v(dst, src):
+            nc.vector.tensor_copy(out=dst, in_=src)
 
         def put_s(page, lst, src):
-            nc.scalar.activation(out=page[:].indirect(lst[:]), in_=src[:], func=COPY)
+            nc.scalar.activation(out=page[:].indirect(lst[:]), in_=src, func=COPY)
 
         def put_v(page, lst, src):
-            nc.vector.tensor_copy(out=page[:].indirect(lst[:]), in_=src[:])
+            nc.vector.tensor_copy(out=page[:].indirect(lst[:]), in_=src)
 
         hid_t = hid[:].rearrange("p (o t) -> p t o", t=PACK)
 
-        def read_board(t):
-            nc.vector.tensor_tensor(out=pg[t][:], in0=pw[t][:], in1=pv[t][:], op=ADD)
-            nc.vector.tensor_copy(out=hid_t[:, t, :], in_=pg[t][:].indirect(l_hid[:]))
+        def add_boards(engine, t):
+            engine.tensor_tensor(out=pg[t][:], in0=pw[t][:], in1=pv[t][:], op=ADD)
 
-        def drain_v(dst, src):
-            nc.vector.tensor_copy(out=dst[:], in_=src[:])
+        def read_board(t, first=0, last=O):
+            nc.vector.tensor_copy(out=hid_t[:, t, first:last], in_=pg[t][:].indirect(l_hid[:, first // 16 : last // 16]))
 
-        drain_s(b_sb[0], b_ps[0])
-        drain_v(b_sb[1], b_ps[1])
-        put_s(pv[0], l_b, b_sb[0])
-        put_v(pv[1], l_b, b_sb[1])
-        drain_s(b_sb[2], b_ps[2])
-        put_s(pv[2], l_b, b_sb[2])
         nc.vector.tensor_copy(out=xtg_s[:], in_=xt_s[:].indirect(l_xt[:]))
-        a_ps = [first_product("a_ps%d" % t, t, xtg_w[:].bitcast(E4M3), xtg_s[:]) for t in range(PACK)]
-        drain_v(b_sb[3], b_ps[3])
-        drain_v(a_sb[0], a_ps[0])
-        put_v(pw[0], l_a, a_sb[0])
-        put_s(pv[3], l_b, b_sb[3])
+        drain_s(b_sb[0][:], b_ps[0][:])
+        drain_s(b_sb[2][:], b_ps[2][:])
+        b_sb[1] = tile("b1", J, F32, tag="xt_s")
+        drain_v(b_sb[1][:], b_ps[1][:])
+        put_s(pv[0], l_b, b_sb[0][:])
+        put_v(pv[1], l_b, b_sb[1][:])
+        put_s(pv[2], l_b, b_sb[2][:])
+        a_ps = [first_product("a_ps%d" % t, "a_ps%d" % t, t, xtg_w[:].bitcast(E4M3), xtg_s[:]) for t in range(PACK)]
+        drain_v(a_sb[0][:], a_ps[0][:])
+        b_ps.append(first_product("b_ps3", "a_ps0", 3, xog_w[:].bitcast(E2M1), xog_s[:]))
+        drain_v(a_sb[1][:], a_ps[1][:])
+        put_v(pw[0], l_a, a_sb[0][:])
+        add_boards(nc.gpsimd, 0)
+        drain_s(a_sb[2][:], a_ps[2][:])
+        drain_s(a_sb[3][:], a_ps[3][:])
+        put_s(pw[2], l_a, a_sb[2][:])
+        add_boards(nc.gpsimd, 2)
+        put_v(pw[1], l_a, a_sb[1][:])
+        drain_s(b_sb[3][:], b_ps[3][:])
+        put_s(pw[3], l_a, a_sb[3][:])
+        put_s(pv[3], l_b, b_sb[3][:])
         read_board(0)
-        drain_s(a_sb[1], a_ps[1])
-        drain_s(a_sb[2], a_ps[2])
-        put_s(pw[2], l_a, a_sb[2])
-        put_v(pw[1], l_a, a_sb[1])
-        read_board(1)
-        drain_s(a_sb[3], a_ps[3])
-        put_s(pw[3], l_a, a_sb[3])
+        add_boards(nc.vector, 1)
         read_board(2)
-        read_board(3)
-
-        nc.vector.quantize_mx(out=hq_w[:].bitcast(E4M3), scales=hq_s[:], in_=hid[:])
-
-        for h in range(N // P):
-            cols = slice(P * h, P * (h + 1))
-            y_ps = ps.tile([P, O], F32, name="y_ps%d" % h, tag="b_ps%d" % h)
-            nc.tensor.matmul_mx(
-                out=y_ps[:], lhsT=wb_w[:, cols].bitcast(E5M2), lhsT_scale=wb_s[:, cols],
-                rhs=hq_w[:].bitcast(E4M3), rhs_scale=hq_s[:], start=True, stop=True,
+        read_board(1)
+        add_boards(nc.vector, 3)
+        halves = [(P * u, P * (u + 1)) for u in range(O // P)]
+        for first, last in halves:
+            read_board(3, first, last)
+        for first, last in halves:
+            nc.vector.quantize_mx(
+                out=hq_w[:, first:last].bitcast(E4M3), scales=hq_s[:, first:last], in_=hid[:, PACK * first : PACK * last]
             )
-            y_sb = tile("y%d" % h, O, F32)
-            if h == 0:
-                nc.vector.tensor_copy(out=y_sb[:], in_=y_ps[:])
-                nc.sync.dma_start(out=out[cols, :], in_=y_sb[:])
-            else:
-                drain_s(y_sb, y_ps)
-                nc.scalar.dma_start(out=out[cols, :], in_=y_sb[:])
+
+        y_sb = [tile("y%d" % h, O, F32) for h in range(N // P)]
+        drains = (drain_v, drain_s)
+        banks = ("b_ps0", "b_ps1", "b_ps2", "a_ps1")
+        for u, (first, last) in enumerate(halves):
+            for h in range(N // P):
+                cols = slice(P * h, P * (h + 1))
+                y_ps = ps.tile([P, P], F32, name="y_ps%d%d" % (u, h), tag=banks[2 * u + h])
+                nc.tensor.matmul_mx(
+                    out=y_ps[:], lhsT=wb_w[:, cols].bitcast(E5M2), lhsT_scale=wb_s[:, cols],
+                    rhs=hq_w[:, first:last].bitcast(E4M3), rhs_scale=hq_s[:, first:last], start=True, stop=True,
+                )
+                drains[h](y_sb[h][:, first:last], y_ps[:])
+        for h, queue in enumerate((nc.sync, nc.scalar)):
+            queue.dma_start(out=out[P * h : P * (h + 1), :], in_=y_sb[h][:])

@@ -46,11 +46,10 @@ def tile_list_oneforboth_shared_one_plain_kernel(
         xtg_w, xtg_s = tile("xtg_w", J, U32), tile("xtg_s", J, U8)
         xog_w, xog_s = tile("xog_w", J, U16), tile("xog_s", J, U8)
         wp_w, wp_s = tile("wp_w", R, U32), tile("wp_s", R, U8)
-        pw = [tile("pw%d" % t, C, F32) for t in range(PACK)]
         pv = [tile("pv%d" % t, C, F32) for t in range(PACK)]
-        pg = [tile("pg%d" % t, C, F32) for t in range(PACK)]
+        pg = [tile("pg%d" % t, C, F32) for t in range(PACK - 1)]
         a_sb = [tile("a%d" % t, J, F32) for t in range(PACK)]
-        b_sb = {t: tile("b%d" % t, J, F32) for t in (0, 2, 3)}
+        b_sb = [tile("b%d" % t, J, F32) for t in range(2)]
         hid = tile("hid", O * PACK, BF16)
         hq_w, hq_s = tile("hq_w", O, U32), tile("hq_s", O, U8)
 
@@ -75,8 +74,8 @@ def tile_list_oneforboth_shared_one_plain_kernel(
         load_words(nc.sync, xt_w, xt_words[0].rearrange("p n t -> p (n t)"))
         nc.sync.dma_start(out=l_xt[:], in_=offs)
         nc.sync.dma_start(out=l_b[:], in_=offs4)
-        for q in range(4):
-            load_scale_rows(nc.sync, xt_s, xt_scales, q)
+        for q, queue in enumerate((nc.sync, nc.gpsimd, nc.gpsimd, nc.gpsimd)):
+            load_scale_rows(queue, xt_s, xt_scales, q)
         nc.sync.dma_start(out=l_a[:], in_=offs3)
         nc.sync.dma_start(out=l_hid[:], in_=offs5)
         load_words(nc.sync, wb_w, wb_words[0].rearrange("p n t -> p (n t)"))
@@ -85,8 +84,6 @@ def tile_list_oneforboth_shared_one_plain_kernel(
 
         for t in range(PACK):
             nc.vector.memset(pv[t][:], 0.0)
-        for t in range(PACK):
-            nc.gpsimd.memset(pw[t][:], 0.0)
 
         nc.vector.tensor_copy(
             out=wp_s[:].rearrange("p (t m) -> p t m", t=PACK),
@@ -97,10 +94,12 @@ def tile_list_oneforboth_shared_one_plain_kernel(
             in_=w_w[:].rearrange("p (g i t) -> p g t i", t=PACK, i=4),
         )
         nc.vector.tensor_copy(out=xog_w[:], in_=xo_w[:].indirect(l_xo[:]))
-        nc.vector.tensor_copy(out=xog_s[:], in_=xo_s[:].indirect(l_xo[:]))
+        half = J // 2
+        nc.vector.tensor_copy(out=xog_s[:, :half], in_=xo_s[:].indirect(l_xo[:, : half // 16]))
+        nc.vector.tensor_copy(out=xog_s[:, half:], in_=xo_s[:].indirect(l_xo[:, half // 16 :]))
 
-        def first_product(name, bank, t, words, scales):
-            acc = ps.tile([P, J], F32, name=name, tag=bank)
+        def first_product(name, t, words, scales, bank=None):
+            acc = ps.tile([P, scales.shape[1]], F32, name=name, tag=bank or name)
             cols = slice(P * t, P * (t + 1))
             nc.tensor.matmul_mx(
                 out=acc[:], lhsT=wp_w[:, cols].bitcast(E5M2), lhsT_scale=wp_s[:, cols],
@@ -108,7 +107,9 @@ def tile_list_oneforboth_shared_one_plain_kernel(
             )
             return acc
 
-        b_ps = [first_product("b_ps%d" % t, "b_ps%d" % t, t, xog_w[:].bitcast(E2M1), xog_s[:]) for t in range(PACK - 1)]
+        b0_lo = first_product("b0_lo", 0, xog_w[:, :half].bitcast(E2M1), xog_s[:, :half], bank="a_ps3")
+        b_ps = [first_product("b_ps0", 0, xog_w[:, half:].bitcast(E2M1), xog_s[:, half:])]
+        b_ps += [first_product("b_ps%d" % t, t, xog_w[:].bitcast(E2M1), xog_s[:]) for t in range(1, PACK)]
 
         nc.vector.tensor_copy(out=xtg_w[:], in_=xt_w[:].indirect(l_xt[:]))
 
@@ -118,8 +119,8 @@ def tile_list_oneforboth_shared_one_plain_kernel(
         def drain_v(dst, src):
             nc.vector.tensor_copy(out=dst, in_=src)
 
-        def put_s(page, lst, src):
-            nc.scalar.activation(out=page[:].indirect(lst[:]), in_=src, func=COPY)
+        def put_s(page, lst, src, first=0, last=J):
+            nc.scalar.activation(out=page[:].indirect(lst[:, first // 16 : last // 16]), in_=src, func=COPY)
 
         def put_v(page, lst, src):
             nc.vector.tensor_copy(out=page[:].indirect(lst[:]), in_=src)
@@ -132,36 +133,50 @@ def tile_list_oneforboth_shared_one_plain_kernel(
         def read_board(t, first=0, last=O):
             nc.vector.tensor_copy(out=hid_t[:, t, first:last], in_=pg[t][:].indirect(l_hid[:, first // 16 : last // 16]))
 
+        drain_s(b_sb[0][:, :half], b0_lo[:])
+        put_s(pv[0], l_b, b_sb[0][:, :half], 0, half)
         nc.vector.tensor_copy(out=xtg_s[:], in_=xt_s[:].indirect(l_xt[:]))
-        drain_s(b_sb[0][:], b_ps[0][:])
-        drain_s(b_sb[2][:], b_ps[2][:])
-        b_sb[1] = tile("b1", J, F32, tag="xt_s")
-        drain_v(b_sb[1][:], b_ps[1][:])
-        put_s(pv[0], l_b, b_sb[0][:])
-        put_v(pv[1], l_b, b_sb[1][:])
-        put_s(pv[2], l_b, b_sb[2][:])
-        a_ps = [first_product("a_ps%d" % t, "a_ps%d" % t, t, xtg_w[:].bitcast(E4M3), xtg_s[:]) for t in range(PACK)]
+        a_ps = [first_product("a_ps%d" % t, t, xtg_w[:].bitcast(E4M3), xtg_s[:]) for t in range(PACK)]
+
+        pw = [tile("pw%d" % t, C, F32, tag=dead) for t, dead in enumerate(("w_w", "xo_w", "xt_w", "wp_w"))]
+        for t in range(PACK):
+            nc.gpsimd.memset(pw[t][:], 0.0)
+
+        drain_s(b_sb[0][:, half:], b_ps[0][:])
+        drain_s(b_sb[1][:], b_ps[1][:])
+        b23 = tile("b23", 2 * J, F32, tag="xt_s")
+        drain_v(b23[:, :J], b_ps[2][:])
+        drain_v(b23[:, J:], b_ps[3][:])
+        put_s(pv[0], l_b, b_sb[0][:, half:], half, J)
+        put_s(pv[1], l_b, b_sb[1][:])
+        put_s(pv[2], l_b, b23[:, :J])
+        put_s(pv[3], l_b, b23[:, J:])
         drain_v(a_sb[0][:], a_ps[0][:])
-        b_ps.append(first_product("b_ps3", "a_ps0", 3, xog_w[:].bitcast(E2M1), xog_s[:]))
         drain_v(a_sb[1][:], a_ps[1][:])
         put_v(pw[0], l_a, a_sb[0][:])
         add_boards(nc.gpsimd, 0)
-        drain_s(a_sb[2][:], a_ps[2][:])
-        drain_s(a_sb[3][:], a_ps[3][:])
-        put_s(pw[2], l_a, a_sb[2][:])
-        add_boards(nc.gpsimd, 2)
+        drain_v(a_sb[2][:], a_ps[2][:])
         put_v(pw[1], l_a, a_sb[1][:])
-        drain_s(b_sb[3][:], b_ps[3][:])
+        add_boards(nc.gpsimd, 1)
+        put_v(pw[2], l_a, a_sb[2][:])
+        add_boards(nc.gpsimd, 2)
+        drain_s(a_sb[3][:], a_ps[3][:])
         put_s(pw[3], l_a, a_sb[3][:])
-        put_s(pv[3], l_b, b_sb[3][:])
         read_board(0)
-        add_boards(nc.vector, 1)
-        read_board(2)
-        read_board(1)
+        hid12 = tile("hid12", 2 * O, BF16)
+        for t in (1, 2):
+            nc.scalar.activation(out=hid12[:, (t - 1) * O : t * O], in_=pg[t][:].indirect(l_hid[:]), func=COPY)
+        pg.append(tile("pg3", C, F32, tag="pg0"))
         add_boards(nc.vector, 3)
+
         halves = [(P * u, P * (u + 1)) for u in range(O // P)]
         for first, last in halves:
             read_board(3, first, last)
+        for first, last in halves:
+            nc.vector.tensor_copy(
+                out=hid[:].rearrange("p (o t) -> p o t", t=PACK)[:, first:last, 1:3],
+                in_=hid12[:].rearrange("p (t o) -> p o t", t=2)[:, first:last, :],
+            )
         for first, last in halves:
             nc.vector.quantize_mx(
                 out=hq_w[:, first:last].bitcast(E4M3), scales=hq_s[:, first:last], in_=hid[:, PACK * first : PACK * last]
@@ -169,7 +184,7 @@ def tile_list_oneforboth_shared_one_plain_kernel(
 
         y_sb = [tile("y%d" % h, O, F32) for h in range(N // P)]
         drains = (drain_v, drain_s)
-        banks = ("b_ps0", "b_ps1", "b_ps2", "a_ps1")
+        banks = ("b_ps0", "b_ps1", "b_ps2", "b_ps3")
         for u, (first, last) in enumerate(halves):
             for h in range(N // P):
                 cols = slice(P * h, P * (h + 1))

@@ -82,8 +82,9 @@ def tile_list_oneforboth_shared_one_plain_kernel(
         for q in range(4):
             load_scale_rows(nc.sync, wb_s, wb_scales, q)
 
-        for t in range(PACK):
-            nc.vector.memset(pv[t][:], 0.0)
+        pw3 = tile("pw3", C, F32)
+        for page in pv + [pw3]:
+            nc.vector.memset(page[:], 0.0)
 
         nc.vector.tensor_copy(
             out=wp_s[:].rearrange("p (t m) -> p t m", t=PACK),
@@ -125,22 +126,31 @@ def tile_list_oneforboth_shared_one_plain_kernel(
         def put_v(page, lst, src):
             nc.vector.tensor_copy(out=page[:].indirect(lst[:]), in_=src)
 
-        hid_t = hid[:].rearrange("p (o t) -> p t o", t=PACK)
+        def add_boards(t):
+            nc.vector.tensor_tensor(out=pg[t][:], in0=pw[t][:], in1=pv[t][:], op=ADD)
 
-        def add_boards(engine, t):
-            engine.tensor_tensor(out=pg[t][:], in0=pw[t][:], in1=pv[t][:], op=ADD)
+        hid_rows = tile("hid_rows", PACK * O, BF16)
 
-        def read_board(t, first=0, last=O):
-            nc.vector.tensor_copy(out=hid_t[:, t, first:last], in_=pg[t][:].indirect(l_hid[:, first // 16 : last // 16]))
+        def read_s(t, first, last):
+            nc.scalar.activation(
+                out=hid_rows[:, t * O + first : t * O + last],
+                in_=pg[t][:].indirect(l_hid[:, first // 16 : last // 16]), func=COPY,
+            )
+
+        def read_v(t, first, last):
+            nc.vector.tensor_copy(
+                out=hid_rows[:, t * O + first : t * O + last], in_=pg[t][:].indirect(l_hid[:, first // 16 : last // 16])
+            )
 
         drain_s(b_sb[0][:, :half], b0_lo[:])
         put_s(pv[0], l_b, b_sb[0][:, :half], 0, half)
         nc.vector.tensor_copy(out=xtg_s[:], in_=xt_s[:].indirect(l_xt[:]))
         a_ps = [first_product("a_ps%d" % t, t, xtg_w[:].bitcast(E4M3), xtg_s[:]) for t in range(PACK)]
 
-        pw = [tile("pw%d" % t, C, F32, tag=dead) for t, dead in enumerate(("w_w", "xo_w", "xt_w", "wp_w"))]
-        for t in range(PACK):
-            nc.gpsimd.memset(pw[t][:], 0.0)
+        pw = [tile("pw%d" % t, C, F32, tag=dead) for t, dead in enumerate(("w_w", "xo_w", "xt_w"))]
+        for page in pw:
+            nc.gpsimd.memset(page[:], 0.0)
+        pw.append(pw3)
 
         drain_s(b_sb[0][:, half:], b_ps[0][:])
         drain_s(b_sb[1][:], b_ps[1][:])
@@ -154,28 +164,28 @@ def tile_list_oneforboth_shared_one_plain_kernel(
         drain_v(a_sb[0][:], a_ps[0][:])
         drain_v(a_sb[1][:], a_ps[1][:])
         put_v(pw[0], l_a, a_sb[0][:])
-        add_boards(nc.gpsimd, 0)
         drain_v(a_sb[2][:], a_ps[2][:])
         put_v(pw[1], l_a, a_sb[1][:])
-        add_boards(nc.gpsimd, 1)
+        add_boards(0)
         put_v(pw[2], l_a, a_sb[2][:])
-        add_boards(nc.gpsimd, 2)
+        add_boards(1)
+        add_boards(2)
         drain_s(a_sb[3][:], a_ps[3][:])
         put_s(pw[3], l_a, a_sb[3][:])
-        read_board(0)
-        hid12 = tile("hid12", 2 * O, BF16)
-        for t in (1, 2):
-            nc.scalar.activation(out=hid12[:, (t - 1) * O : t * O], in_=pg[t][:].indirect(l_hid[:]), func=COPY)
-        pg.append(tile("pg3", C, F32, tag="pg0"))
-        add_boards(nc.vector, 3)
+        read_s(0, 0, O)
+        read_s(1, 0, O)
+        read_s(2, P, O)
+        pg.append(tile("pg3", C, F32, tag="a2"))
+        add_boards(3)
+        read_v(2, 0, P)
 
         halves = [(P * u, P * (u + 1)) for u in range(O // P)]
         for first, last in halves:
-            read_board(3, first, last)
+            read_v(3, first, last)
         for first, last in halves:
             nc.vector.tensor_copy(
-                out=hid[:].rearrange("p (o t) -> p o t", t=PACK)[:, first:last, 1:3],
-                in_=hid12[:].rearrange("p (t o) -> p o t", t=2)[:, first:last, :],
+                out=hid[:, PACK * first : PACK * last].rearrange("p (g i t) -> p g t i", i=4, t=PACK),
+                in_=hid_rows[:].rearrange("p (t g i) -> p g t i", t=PACK, i=4)[:, first // 4 : last // 4],
             )
         for first, last in halves:
             nc.vector.quantize_mx(

@@ -19,6 +19,11 @@ ADD = mybir.AluOpType.add
 
 P = 128
 PACK = 4
+QUADRANT = 32
+QUADRANTS = P // QUADRANT
+ROWS = 4
+PER_COLUMN = 16
+RUN = 4
 
 
 def tile_list_oneforboth_shared_one_plain_kernel(
@@ -33,11 +38,14 @@ def tile_list_oneforboth_shared_one_plain_kernel(
         def tile(name, cols, dtype, tag=None):
             return sb.tile([P, cols], dtype, name=name, tag=tag or name, align_bytes=64)
 
-        l_xt = tile("l_xt", J // 16, U16)
-        l_xo = tile("l_xo", J // 16, U16)
-        l_a = tile("l_a", J // 16, U16)
-        l_b = tile("l_b", J // 16, U16)
-        l_hid = tile("l_hid", O // 16, U16)
+        def entries(list_tile, first, last):
+            return list_tile[:, first // PER_COLUMN : last // PER_COLUMN]
+
+        l_xt = tile("l_xt", J // PER_COLUMN, U16)
+        l_xo = tile("l_xo", J // PER_COLUMN, U16)
+        l_a = tile("l_a", J // PER_COLUMN, U16)
+        l_b = tile("l_b", J // PER_COLUMN, U16)
+        l_hid = tile("l_hid", O // PER_COLUMN, U16)
 
         xt_w, xt_s = tile("xt_w", T, U32), tile("xt_s", T, U8)
         xo_w, xo_s = tile("xo_w", Z, U16), tile("xo_s", Z, U8)
@@ -53,51 +61,58 @@ def tile_list_oneforboth_shared_one_plain_kernel(
         hid = tile("hid", O * PACK, BF16)
         hq_w, hq_s = tile("hq_w", O, U32), tile("hq_s", O, U8)
 
-        def load_words(queue, dst, src):
-            queue.dma_start(out=dst[:].bitcast(I32), in_=src.bitcast(I32))
+        def load_words(dst, src):
+            nc.sync.dma_start(out=dst[:].bitcast(I32), in_=src.bitcast(I32))
 
-        def load_scale_rows(queue, dst, src, q):
-            rows = src[0, 4 * q : 4 * q + 4, :].bitcast(I32)
+        def scale_rows(src, q):
+            return src[0, ROWS * q : ROWS * (q + 1), :].bitcast(I32)
+
+        def load_rows_repeated(queue, dst, src, q):
+            rows = scale_rows(src, q)
             queue.dma_start(
-                out=dst[32 * q : 32 * (q + 1), :].bitcast(I32),
-                in_=rows.unsqueeze(0).broadcast_to([8, 4, rows.shape[1]]),
+                out=dst[QUADRANT * q : QUADRANT * (q + 1), :].bitcast(I32),
+                in_=rows.unsqueeze(0).broadcast_to([QUADRANT // ROWS, ROWS, rows.shape[1]]),
             )
 
+        def load_rows_once(queue, dst, src, q):
+            queue.dma_start(out=dst[QUADRANT * q : QUADRANT * q + ROWS, :].bitcast(I32), in_=scale_rows(src, q))
+
+        for plane in (xt_s, wb_s):
+            nc.vector.memset(plane[:].bitcast(I32), 0)
+
         nc.sync.dma_start(out=l_xo[:], in_=offs2)
-        for q in range(4):
-            load_scale_rows(nc.scalar, w_s, w_scales, q)
-        load_scale_rows(nc.sync, xo_s, xo_scales, 0)
-        load_words(nc.sync, w_w, w_words[0].rearrange("p n t -> p (n t)"))
-        load_words(nc.sync, xo_w, xo_words[0])
-        for q in range(1, 4):
-            load_scale_rows(nc.sync, xo_s, xo_scales, q)
-        load_words(nc.sync, xt_w, xt_words[0].rearrange("p n t -> p (n t)"))
+        for q in range(QUADRANTS):
+            load_rows_repeated(nc.scalar, xo_s, xo_scales, q)
+        load_rows_repeated(nc.sync, w_s, w_scales, 0)
+        load_words(w_w, w_words[0].rearrange("p n t -> p (n t)"))
+        load_words(xo_w, xo_words[0])
+        for q in range(1, QUADRANTS):
+            load_rows_repeated(nc.sync, w_s, w_scales, q)
+        load_words(xt_w, xt_words[0].rearrange("p n t -> p (n t)"))
         nc.sync.dma_start(out=l_xt[:], in_=offs)
         nc.sync.dma_start(out=l_b[:], in_=offs4)
-        for q, queue in enumerate((nc.sync, nc.gpsimd, nc.gpsimd, nc.gpsimd)):
-            load_scale_rows(queue, xt_s, xt_scales, q)
+        for q, queue in enumerate((nc.sync, nc.sync, nc.gpsimd, nc.gpsimd)):
+            load_rows_once(queue, xt_s, xt_scales, q)
         nc.sync.dma_start(out=l_a[:], in_=offs3)
         nc.sync.dma_start(out=l_hid[:], in_=offs5)
-        load_words(nc.sync, wb_w, wb_words[0].rearrange("p n t -> p (n t)"))
-        for q in range(4):
-            load_scale_rows(nc.sync, wb_s, wb_scales, q)
+        load_words(wb_w, wb_words[0].rearrange("p n t -> p (n t)"))
+        for q in range(QUADRANTS):
+            load_rows_once(nc.sync, wb_s, wb_scales, q)
 
-        pw3 = tile("pw3", C, F32)
-        for page in pv + [pw3]:
-            nc.vector.memset(page[:], 0.0)
+        for board in pv:
+            nc.vector.memset(board[:], 0.0)
 
+        nc.vector.tensor_copy(out=xog_s[:], in_=xo_s[:].indirect(l_xo[:]))
         nc.vector.tensor_copy(
-            out=wp_s[:].rearrange("p (t m) -> p t m", t=PACK),
-            in_=w_s[:].rearrange("p (m t) -> p t m", t=PACK),
-        )
-        nc.vector.tensor_copy(
-            out=wp_w[:].rearrange("p (t g i) -> p g t i", t=PACK, i=4),
-            in_=w_w[:].rearrange("p (g i t) -> p g t i", t=PACK, i=4),
+            out=wp_w[:].rearrange("p (t g i) -> p g t i", t=PACK, i=RUN),
+            in_=w_w[:].rearrange("p (g i t) -> p g t i", t=PACK, i=RUN),
         )
         nc.vector.tensor_copy(out=xog_w[:], in_=xo_w[:].indirect(l_xo[:]))
-        half = J // 2
-        nc.vector.tensor_copy(out=xog_s[:, :half], in_=xo_s[:].indirect(l_xo[:, : half // 16]))
-        nc.vector.tensor_copy(out=xog_s[:, half:], in_=xo_s[:].indirect(l_xo[:, half // 16 :]))
+        for first, last in ((0, 1), (1, PACK)):
+            nc.vector.tensor_copy(
+                out=wp_s[:].rearrange("p (t m) -> p t m", t=PACK)[:, first:last],
+                in_=w_s[:].rearrange("p (m t) -> p t m", t=PACK)[:, first:last],
+            )
 
         def first_product(name, t, words, scales, bank=None):
             acc = ps.tile([P, scales.shape[1]], F32, name=name, tag=bank or name)
@@ -108,6 +123,7 @@ def tile_list_oneforboth_shared_one_plain_kernel(
             )
             return acc
 
+        half = J // 2
         b0_lo = first_product("b0_lo", 0, xog_w[:, :half].bitcast(E2M1), xog_s[:, :half], bank="a_ps3")
         b_ps = [first_product("b_ps0", 0, xog_w[:, half:].bitcast(E2M1), xog_s[:, half:])]
         b_ps += [first_product("b_ps%d" % t, t, xog_w[:].bitcast(E2M1), xog_s[:]) for t in range(1, PACK)]
@@ -120,11 +136,11 @@ def tile_list_oneforboth_shared_one_plain_kernel(
         def drain_v(dst, src):
             nc.vector.tensor_copy(out=dst, in_=src)
 
-        def put_s(page, lst, src, first=0, last=J):
-            nc.scalar.activation(out=page[:].indirect(lst[:, first // 16 : last // 16]), in_=src, func=COPY)
+        def put_s(board, list_tile, src, first=0, last=J):
+            nc.scalar.activation(out=board[:].indirect(entries(list_tile, first, last)), in_=src, func=COPY)
 
-        def put_v(page, lst, src):
-            nc.vector.tensor_copy(out=page[:].indirect(lst[:]), in_=src)
+        def put_v(board, list_tile, src):
+            nc.vector.tensor_copy(out=board[:].indirect(list_tile[:]), in_=src)
 
         def add_boards(t):
             nc.vector.tensor_tensor(out=pg[t][:], in0=pw[t][:], in1=pv[t][:], op=ADD)
@@ -134,12 +150,12 @@ def tile_list_oneforboth_shared_one_plain_kernel(
         def read_s(t, first, last):
             nc.scalar.activation(
                 out=hid_rows[:, t * O + first : t * O + last],
-                in_=pg[t][:].indirect(l_hid[:, first // 16 : last // 16]), func=COPY,
+                in_=pg[t][:].indirect(entries(l_hid, first, last)), func=COPY,
             )
 
         def read_v(t, first, last):
             nc.vector.tensor_copy(
-                out=hid_rows[:, t * O + first : t * O + last], in_=pg[t][:].indirect(l_hid[:, first // 16 : last // 16])
+                out=hid_rows[:, t * O + first : t * O + last], in_=pg[t][:].indirect(entries(l_hid, first, last))
             )
 
         drain_s(b_sb[0][:, :half], b0_lo[:])
@@ -147,10 +163,9 @@ def tile_list_oneforboth_shared_one_plain_kernel(
         nc.vector.tensor_copy(out=xtg_s[:], in_=xt_s[:].indirect(l_xt[:]))
         a_ps = [first_product("a_ps%d" % t, t, xtg_w[:].bitcast(E4M3), xtg_s[:]) for t in range(PACK)]
 
-        pw = [tile("pw%d" % t, C, F32, tag=dead) for t, dead in enumerate(("w_w", "xo_w", "xt_w"))]
-        for page in pw:
-            nc.gpsimd.memset(page[:], 0.0)
-        pw.append(pw3)
+        pw = [tile("pw%d" % t, C, F32, tag=dead) for t, dead in enumerate(("w_s", "xt_w", "xog_w", "xog_s"))]
+        for board in pw:
+            nc.gpsimd.memset(board[:], 0.0)
 
         drain_s(b_sb[0][:, half:], b_ps[0][:])
         drain_s(b_sb[1][:], b_ps[1][:])
@@ -172,20 +187,20 @@ def tile_list_oneforboth_shared_one_plain_kernel(
         add_boards(2)
         drain_s(a_sb[3][:], a_ps[3][:])
         put_s(pw[3], l_a, a_sb[3][:])
+        halves = [(P * u, P * (u + 1)) for u in range(O // P)]
         read_s(0, 0, O)
         read_s(1, 0, O)
-        read_s(2, P, O)
+        read_s(2, *halves[1])
         pg.append(tile("pg3", C, F32, tag="a2"))
         add_boards(3)
-        read_v(2, 0, P)
+        read_v(2, *halves[0])
 
-        halves = [(P * u, P * (u + 1)) for u in range(O // P)]
         for first, last in halves:
             read_v(3, first, last)
         for first, last in halves:
             nc.vector.tensor_copy(
-                out=hid[:, PACK * first : PACK * last].rearrange("p (g i t) -> p g t i", i=4, t=PACK),
-                in_=hid_rows[:].rearrange("p (t g i) -> p g t i", t=PACK, i=4)[:, first // 4 : last // 4],
+                out=hid[:, PACK * first : PACK * last].rearrange("p (g i t) -> p g t i", i=RUN, t=PACK),
+                in_=hid_rows[:].rearrange("p (t g i) -> p g t i", t=PACK, i=RUN)[:, first // RUN : last // RUN],
             )
         for first, last in halves:
             nc.vector.quantize_mx(
@@ -194,15 +209,14 @@ def tile_list_oneforboth_shared_one_plain_kernel(
 
         y_sb = [tile("y%d" % h, O, F32) for h in range(N // P)]
         drains = (drain_v, drain_s)
-        banks = ("b_ps0", "b_ps1", "b_ps2", "b_ps3")
         for u, (first, last) in enumerate(halves):
             for h in range(N // P):
                 cols = slice(P * h, P * (h + 1))
-                y_ps = ps.tile([P, P], F32, name="y_ps%d%d" % (u, h), tag=banks[2 * u + h])
+                y_ps = ps.tile([P, P], F32, name="y_ps%d%d" % (u, h), tag="b_ps%d" % (2 * u + h))
                 nc.tensor.matmul_mx(
                     out=y_ps[:], lhsT=wb_w[:, cols].bitcast(E5M2), lhsT_scale=wb_s[:, cols],
                     rhs=hq_w[:, first:last].bitcast(E4M3), rhs_scale=hq_s[:, first:last], start=True, stop=True,
                 )
                 drains[h](y_sb[h][:, first:last], y_ps[:])
-        for h, queue in enumerate((nc.sync, nc.scalar)):
-            queue.dma_start(out=out[P * h : P * (h + 1), :], in_=y_sb[h][:])
+                queue = nc.scalar if (u, h) == (1, 1) else nc.sync
+                queue.dma_start(out=out[cols, first:last], in_=y_sb[h][:, first:last])

from contextlib import ExitStack

import concourse.mybir as mybir

K, T, Z, J, R, C, O, N = 512, 1024, 1024, 256, 512, 512, 256, 256
FLOPS = 2 * (2 * K * R * J + R * N * O)

F32 = mybir.dt.float32
BF16 = mybir.dt.bfloat16
I32 = mybir.dt.int32
U32 = mybir.dt.uint32
U16 = mybir.dt.uint16
U8 = mybir.dt.uint8
E4M3 = mybir.dt.float8_e4m3fn_x4
E5M2 = mybir.dt.float8_e5m2_x4
E2M1 = mybir.dt.float4_e2m1fn_x4
COPY = mybir.ActivationFunctionType.Copy
ADD = mybir.AluOpType.add

P = 128
PACK = 4
QUADRANT = 32
QUADRANTS = P // QUADRANT
ROWS = 4
PER_COLUMN = 16
RUN = 4


def tile_list_oneforboth_shared_one_plain_kernel(
    tc, xt_words, xt_scales, xo_words, xo_scales, w_words, w_scales, wb_words, wb_scales,
    offs, offs2, offs3, offs4, offs5, out,
):
    nc = tc.nc
    with ExitStack() as ctx:
        sb = ctx.enter_context(tc.tile_pool(name="sb", bufs=1))
        ps = ctx.enter_context(tc.psum_pool(name="ps", bufs=1))

        def tile(name, cols, dtype, tag=None):
            return sb.tile([P, cols], dtype, name=name, tag=tag or name, align_bytes=64)

        def entries(list_tile, first, last):
            return list_tile[:, first // PER_COLUMN : last // PER_COLUMN]

        l_xt = tile("l_xt", J // PER_COLUMN, U16)
        l_xo = tile("l_xo", J // PER_COLUMN, U16)
        l_a = tile("l_a", J // PER_COLUMN, U16)
        l_b = tile("l_b", J // PER_COLUMN, U16)
        l_hid = tile("l_hid", O // PER_COLUMN, U16)

        xt_w, xt_s = tile("xt_w", T, U32), tile("xt_s", T, U8)
        xo_w, xo_s = tile("xo_w", Z, U16), tile("xo_s", Z, U8)
        w_w, w_s = tile("w_w", R, U32), tile("w_s", R, U8)
        wb_w, wb_s = tile("wb_w", N, U32), tile("wb_s", N, U8)
        xtg_w, xtg_s = tile("xtg_w", J, U32), tile("xtg_s", J, U8)
        xog_w, xog_s = tile("xog_w", J, U16), tile("xog_s", J, U8)
        wp_w, wp_s = tile("wp_w", R, U32), tile("wp_s", R, U8)
        pv = [tile("pv%d" % t, C, F32) for t in range(PACK)]
        pg = [tile("pg%d" % t, C, F32) for t in range(PACK - 1)]
        a_sb = [tile("a%d" % t, J, F32) for t in range(PACK)]
        b_sb = [tile("b%d" % t, J, F32) for t in range(2)]
        hid = tile("hid", O * PACK, BF16)
        hq_w, hq_s = tile("hq_w", O, U32), tile("hq_s", O, U8)

        def load_words(dst, src):
            nc.sync.dma_start(out=dst[:].bitcast(I32), in_=src.bitcast(I32))

        def scale_rows(src, q):
            return src[0, ROWS * q : ROWS * (q + 1), :].bitcast(I32)

        def load_rows_repeated(queue, dst, src, q):
            rows = scale_rows(src, q)
            queue.dma_start(
                out=dst[QUADRANT * q : QUADRANT * (q + 1), :].bitcast(I32),
                in_=rows.unsqueeze(0).broadcast_to([QUADRANT // ROWS, ROWS, rows.shape[1]]),
            )

        def load_rows_once(queue, dst, src, q):
            queue.dma_start(out=dst[QUADRANT * q : QUADRANT * q + ROWS, :].bitcast(I32), in_=scale_rows(src, q))

        for plane in (xt_s, wb_s):
            nc.vector.memset(plane[:].bitcast(I32), 0)

        nc.sync.dma_start(out=l_xo[:], in_=offs2)
        for q in range(QUADRANTS):
            load_rows_repeated(nc.scalar, xo_s, xo_scales, q)
        load_rows_repeated(nc.sync, w_s, w_scales, 0)
        load_words(w_w, w_words[0].rearrange("p n t -> p (n t)"))
        load_words(xo_w, xo_words[0])
        for q in range(1, QUADRANTS):
            load_rows_repeated(nc.sync, w_s, w_scales, q)
        load_words(xt_w, xt_words[0].rearrange("p n t -> p (n t)"))
        nc.sync.dma_start(out=l_xt[:], in_=offs)
        nc.sync.dma_start(out=l_b[:], in_=offs4)
        for q, queue in enumerate((nc.sync, nc.sync, nc.gpsimd, nc.gpsimd)):
            load_rows_once(queue, xt_s, xt_scales, q)
        nc.sync.dma_start(out=l_a[:], in_=offs3)
        nc.sync.dma_start(out=l_hid[:], in_=offs5)
        load_words(wb_w, wb_words[0].rearrange("p n t -> p (n t)"))
        for q in range(QUADRANTS):
            load_rows_once(nc.sync, wb_s, wb_scales, q)

        for board in pv:
            nc.vector.memset(board[:], 0.0)

        nc.vector.tensor_copy(out=xog_s[:], in_=xo_s[:].indirect(l_xo[:]))
        nc.vector.tensor_copy(
            out=wp_w[:].rearrange("p (t g i) -> p g t i", t=PACK, i=RUN),
            in_=w_w[:].rearrange("p (g i t) -> p g t i", t=PACK, i=RUN),
        )
        nc.vector.tensor_copy(out=xog_w[:], in_=xo_w[:].indirect(l_xo[:]))
        for first, last in ((0, 1), (1, PACK)):
            nc.vector.tensor_copy(
                out=wp_s[:].rearrange("p (t m) -> p t m", t=PACK)[:, first:last],
                in_=w_s[:].rearrange("p (m t) -> p t m", t=PACK)[:, first:last],
            )

        def first_product(name, t, words, scales, bank=None):
            acc = ps.tile([P, scales.shape[1]], F32, name=name, tag=bank or name)
            cols = slice(P * t, P * (t + 1))
            nc.tensor.matmul_mx(
                out=acc[:], lhsT=wp_w[:, cols].bitcast(E5M2), lhsT_scale=wp_s[:, cols],
                rhs=words, rhs_scale=scales, start=True, stop=True,
            )
            return acc

        half = J // 2
        b0_lo = first_product("b0_lo", 0, xog_w[:, :half].bitcast(E2M1), xog_s[:, :half], bank="a_ps3")
        b_ps = [first_product("b_ps0", 0, xog_w[:, half:].bitcast(E2M1), xog_s[:, half:])]
        b_ps += [first_product("b_ps%d" % t, t, xog_w[:].bitcast(E2M1), xog_s[:]) for t in range(1, PACK)]

        nc.vector.tensor_copy(out=xtg_w[:], in_=xt_w[:].indirect(l_xt[:]))

        def drain_s(dst, src):
            nc.scalar.activation(out=dst, in_=src, func=COPY)

        def drain_v(dst, src):
            nc.vector.tensor_copy(out=dst, in_=src)

        def put_s(board, list_tile, src, first=0, last=J):
            nc.scalar.activation(out=board[:].indirect(entries(list_tile, first, last)), in_=src, func=COPY)

        def put_v(board, list_tile, src):
            nc.vector.tensor_copy(out=board[:].indirect(list_tile[:]), in_=src)

        def add_boards(t):
            nc.vector.tensor_tensor(out=pg[t][:], in0=pw[t][:], in1=pv[t][:], op=ADD)

        hid_rows = tile("hid_rows", PACK * O, BF16)

        def read_s(t, first, last):
            nc.scalar.activation(
                out=hid_rows[:, t * O + first : t * O + last],
                in_=pg[t][:].indirect(entries(l_hid, first, last)), func=COPY,
            )

        def read_v(t, first, last):
            nc.vector.tensor_copy(
                out=hid_rows[:, t * O + first : t * O + last], in_=pg[t][:].indirect(entries(l_hid, first, last))
            )

        drain_s(b_sb[0][:, :half], b0_lo[:])
        put_s(pv[0], l_b, b_sb[0][:, :half], 0, half)
        nc.vector.tensor_copy(out=xtg_s[:], in_=xt_s[:].indirect(l_xt[:]))
        a_ps = [first_product("a_ps%d" % t, t, xtg_w[:].bitcast(E4M3), xtg_s[:]) for t in range(PACK)]

        pw = [tile("pw%d" % t, C, F32, tag=dead) for t, dead in enumerate(("w_s", "xt_w", "xog_w", "xog_s"))]
        for board in pw:
            nc.gpsimd.memset(board[:], 0.0)

        drain_s(b_sb[0][:, half:], b_ps[0][:])
        drain_s(b_sb[1][:], b_ps[1][:])
        b23 = tile("b23", 2 * J, F32, tag="xt_s")
        drain_v(b23[:, :J], b_ps[2][:])
        drain_v(b23[:, J:], b_ps[3][:])
        put_s(pv[0], l_b, b_sb[0][:, half:], half, J)
        put_s(pv[1], l_b, b_sb[1][:])
        put_s(pv[2], l_b, b23[:, :J])
        put_s(pv[3], l_b, b23[:, J:])
        drain_v(a_sb[0][:], a_ps[0][:])
        drain_v(a_sb[1][:], a_ps[1][:])
        put_v(pw[0], l_a, a_sb[0][:])
        drain_v(a_sb[2][:], a_ps[2][:])
        put_v(pw[1], l_a, a_sb[1][:])
        add_boards(0)
        put_v(pw[2], l_a, a_sb[2][:])
        add_boards(1)
        add_boards(2)
        drain_s(a_sb[3][:], a_ps[3][:])
        put_s(pw[3], l_a, a_sb[3][:])
        halves = [(P * u, P * (u + 1)) for u in range(O // P)]
        read_s(0, 0, O)
        read_s(1, 0, O)
        read_s(2, *halves[1])
        pg.append(tile("pg3", C, F32, tag="a2"))
        add_boards(3)
        read_v(2, *halves[0])

        for first, last in halves:
            read_v(3, first, last)
        for first, last in halves:
            nc.vector.tensor_copy(
                out=hid[:, PACK * first : PACK * last].rearrange("p (g i t) -> p g t i", i=RUN, t=PACK),
                in_=hid_rows[:].rearrange("p (t g i) -> p g t i", t=PACK, i=RUN)[:, first // RUN : last // RUN],
            )
        for first, last in halves:
            nc.vector.quantize_mx(
                out=hq_w[:, first:last].bitcast(E4M3), scales=hq_s[:, first:last], in_=hid[:, PACK * first : PACK * last]
            )

        y_sb = [tile("y%d" % h, O, F32) for h in range(N // P)]
        drains = (drain_v, drain_s)
        for u, (first, last) in enumerate(halves):
            for h in range(N // P):
                cols = slice(P * h, P * (h + 1))
                y_ps = ps.tile([P, P], F32, name="y_ps%d%d" % (u, h), tag="b_ps%d" % (2 * u + h))
                nc.tensor.matmul_mx(
                    out=y_ps[:], lhsT=wb_w[:, cols].bitcast(E5M2), lhsT_scale=wb_s[:, cols],
                    rhs=hq_w[:, first:last].bitcast(E4M3), rhs_scale=hq_s[:, first:last], start=True, stop=True,
                )
                drains[h](y_sb[h][:, first:last], y_ps[:])
                queue = nc.scalar if (u, h) == (1, 1) else nc.sync
                queue.dma_start(out=out[cols, first:last], in_=y_sb[h][:, first:last])
